import numpy as np
import ml_dtypes


def mxq(x, axis, fmt="e4m3"):
    dtype, down = {"e4m3": (ml_dtypes.float8_e4m3fn, 7), "e5m2": (ml_dtypes.float8_e5m2, 14)}[fmt]
    v = np.moveaxis(np.asarray(x, np.float32).astype(ml_dtypes.bfloat16).astype(np.float64), axis, -1)
    blocks = v.reshape(v.shape[:-1] + (-1, 32))
    amax = np.abs(blocks).max(-1, keepdims=True)
    byte = np.maximum(np.where(amax > 0, np.frexp(amax)[1] - 1 + 127, 0) - down, 1)
    scale = np.exp2(byte - 127.0)
    codes = (blocks / scale).astype(np.float32).astype(dtype).astype(np.float64)
    return np.moveaxis((codes * scale).reshape(v.shape), -1, axis)


WIDE = False


def mx_kscale(k):
    if not WIDE:
        return np.ones(k)
    levels = np.array([10, -10, 5, -5, 0])
    if k % 512:
        return np.exp2(np.random.permutation(np.resize(levels, k // 32))).repeat(32)
    a = np.empty((k // 512, 16))
    for p in range(k // 512):
        a[p, :8] = np.random.permutation(np.resize(levels, 8))
        for g in range(8):
            far = levels[np.abs(levels - a[p, g]) >= 10]
            a[p, g + 8] = far[np.random.randint(len(far))]
    return np.exp2(a.ravel()).repeat(32)


def f64(x):
    return np.asarray(x).astype(np.float64)


def striped(idx):
    return np.tile(np.asarray(idx).reshape(-1, 16).T, (8, 1)).astype(np.uint16)


def unstriped(offs):
    return offs[:16].T.reshape(-1).astype(np.int64)


E2M1 = np.array([0.0, 0.5, 1.0, 1.5, 2.0, 3.0, 4.0, 6.0, -0.0, -0.5, -1.0, -1.5, -2.0, -3.0, -4.0, -6.0])


def pack_weight(w, fmt):
    k, n = w.shape
    w = f64(np.asarray(w, np.float32).astype(ml_dtypes.bfloat16)).reshape(k // 32, 32, n)
    amax = np.abs(w).max(1)
    if fmt == "e4m3":
        byte = np.frexp(amax)[1] - 1 + 127 - 7
    else:
        mant, ex = np.frexp(amax / 6.0)
        byte = np.where(mant > 0.5, ex, ex - 1) + 127
    byte = np.clip(np.where(amax > 0, byte, 1), 1, 254)
    scaled = (w * np.exp2(127.0 - byte)[:, None, :]).reshape(k, n).astype(np.float32)
    by_word = np.ascontiguousarray(scaled.reshape(k // 512, 128, 4, n).transpose(0, 1, 3, 2))
    if fmt == "e4m3":
        words = by_word.astype(ml_dtypes.float8_e4m3fn).view(np.uint8)
    else:
        c = by_word.astype(ml_dtypes.float4_e2m1fn).view(np.uint8) & 0xF
        words = (c[..., 0::2] | (c[..., 1::2] << 4)).reshape(k // 512, 128, 2 * n)
    return np.ascontiguousarray(words), np.ascontiguousarray(byte.astype(np.uint8).reshape(k // 512, 16, n))


def unpack_weight(words, scales, fmt):
    g, _, n = scales.shape
    words = np.ascontiguousarray(words).reshape(g, 128, n, -1)
    if fmt == "e4m3":
        vals = words.view(ml_dtypes.float8_e4m3fn).astype(np.float64)
    else:
        nib = np.empty((g, 128, n, 4), np.uint8)
        nib[..., 0::2] = words & 0xF
        nib[..., 1::2] = words >> 4
        vals = E2M1[nib]
    vals = vals * np.repeat(np.exp2(scales.astype(np.float64) - 127.0), 8, axis=1)[..., None]
    return vals.transpose(0, 1, 3, 2).reshape(g * 512, n)


def sigmoid(v):
    return 1.0 / (1.0 + np.exp(-v))


D, T, I, Q, E, U, M = 512, 2048, 512, 512, 512, 1024, 1024


def setup_inputs():
    n = np.random.standard_normal
    idx = np.random.permutation(T)[:I]
    idx2 = np.random.permutation(U)[:I]
    idx3 = np.random.permutation(M)[:I]
    fd = mx_kscale(D)
    fq = mx_kscale(Q)
    keysp = pack_weight(n((D, T)) / fd[:, None], "e2m1")
    return {
        "query": (n((D, Q)) * 0.7 / np.sqrt(D) * fd[:, None]).astype(np.float32),
        "query2": (n((D, Q)) * 0.7 / np.sqrt(D) * fd[:, None]).astype(np.float32),
        "keys_words": keysp[0],
        "keys_scales": keysp[1],
        "notes": (n((D, U)) / fd[:, None]).astype(np.float32),
        "qs": (np.random.uniform(0.5, 2.0, (Q, 1)) * fq[:, None]).astype(np.float32),
        "msgs": (n((Q, E)) * 1 / np.sqrt(Q) / fq[:, None]).astype(np.float32),
        "old": (n((E, M)) * 1.0).astype(np.float32),
        "fade": (np.random.uniform(0.3, 0.9, (1, M))).astype(np.float32),
        "offs": striped(idx),
        "offs2": striped(idx2),
        "offs3": striped(idx3),
    }


def reference(query, query2, keys_words, keys_scales, notes, qs, msgs, old, fade, offs, offs2, offs3):
    idx = unstriped(offs)
    idx2 = unstriped(offs2)
    idx3 = unstriped(offs3)
    keysu = unpack_weight(keys_words, keys_scales, "e2m1")
    queryq = mxq(f64(query), 0, "e4m3")
    keysidxg = keysu[:, idx]
    query2q = mxq(f64(query2), 0, "e4m3")
    notesidx2q = mxq(f64(notes)[:, idx2], 0, "e4m3")
    s = queryq.T @ keysidxg + query2q.T @ notesidx2q
    w = sigmoid(s)
    wq = w * f64(qs)
    msgsq = mxq(f64(msgs), 0, "e4m3")
    wqq = mxq(wq, 0, "e4m3")
    dl = msgsq.T @ wqq
    df = np.zeros((E, M))
    df[:, idx3] = dl
    y = f64(old) * f64(fade) + df
    return y

@@ -1,0 +1,232 @@
+from contextlib import ExitStack
+
+import concourse.mybir as mybir
+from concourse.masks import make_identity
+
+D, T, I, Q, E, U, M = 512, 2048, 512, 512, 512, 1024, 1024
+FLOPS = 2 * (2 * D * Q * I + Q * E * I)
+
+F32 = mybir.dt.float32
+BF16 = mybir.dt.bfloat16
+I32 = mybir.dt.int32
+U32 = mybir.dt.uint32
+U16 = mybir.dt.uint16
+U8 = mybir.dt.uint8
+FP8X4 = mybir.dt.float8_e4m3fn_x4
+FP4X4 = mybir.dt.float4_e2m1fn_x4
+MULT = mybir.AluOpType.mult
+ADD = mybir.AluOpType.add
+COPY = mybir.ActivationFunctionType.Copy
+SIGMOID = mybir.ActivationFunctionType.Sigmoid
+
+P = 128
+PACK = 4
+CHUNK = 128
+CHUNKS = I // CHUNK
+HALF = 256
+BANK = 512
+
+
+def tile_attend_twosources_delivered_lean_kernel(
+    tc, query, query2, keys_words, keys_scales, notes, qs, msgs, old, fade, offs, offs2, offs3, out
+):
+    nc = tc.nc
+    with ExitStack() as ctx:
+        sb = ctx.enter_context(tc.tile_pool(name="sb", bufs=1))
+        ps = ctx.enter_context(tc.psum_pool(name="ps", bufs=1))
+        ps2 = ctx.enter_context(tc.psum_pool(name="ps2", bufs=2))
+
+        def tile(shape, dtype, name):
+            return sb.tile(shape, dtype, name=name, align_bytes=64)
+
+        list1 = tile([P, I // 16], U16, "list1")
+        list2 = tile([P, I // 16], U16, "list2")
+        list3 = tile([P, I // 16], U16, "list3")
+        key_words = tile([P, T], U16, "key_words")
+        key_scales = tile([P, T], U8, "key_scales")
+        note_planes = [tile([P, U], F32, f"note_plane{j}") for j in range(PACK)]
+        q2_raw = [tile([P, PACK, HALF], F32, f"q2_raw{h}") for h in range(2)]
+        q_raw = [tile([P, PACK, HALF], F32, f"q_raw{h}") for h in range(2)]
+        m_raw = [tile([P, PACK, HALF], F32, f"m_raw{h}") for h in range(2)]
+        rows = [tile([P, M], F32, f"rows{t}") for t in range(E // P)]
+        windows = [tile([P, M], F32, f"window{t}") for t in range(E // P)]
+        qs4 = tile([P, PACK], F32, "qs4")
+        fade_cols = tile([P, 2, PACK], F32, "fade_cols")
+        ident = tile([P, P], F32, "ident")
+
+        nc.vector.memset(key_scales[:].bitcast(I32), 0)
+        for t in (0, 3):
+            nc.vector.memset(windows[t][:], 0.0)
+        make_identity(nc, ident[:])
+        for t in (1, 2):
+            nc.gpsimd.memset(windows[t][:], 0.0)
+
+        notes_v = notes.rearrange("(p j) u -> p j u", j=PACK)
+        query_v = query.rearrange("(p j) q -> p j q", j=PACK)
+        query2_v = query2.rearrange("(p j) q -> p j q", j=PACK)
+        msgs_v = msgs.rearrange("(p j) e -> p j e", j=PACK)
+        nc.sync.dma_start(list1[:], offs)
+        nc.sync.dma_start(key_words[:].bitcast(I32), keys_words[0].bitcast(I32))
+        nc.sync.dma_start(list2[:], offs2)
+        for j in range(PACK):
+            nc.sync.dma_start(note_planes[j][:], notes_v[:, j, :])
+        for g in range(4):
+            nc.scalar.dma_start(
+                key_scales[32 * g : 32 * g + 4, :].bitcast(I32), keys_scales[0, 4 * g : 4 * g + 4, :].bitcast(I32)
+            )
+        for h in range(2):
+            nc.sync.dma_start(q2_raw[h][:], query2_v[:, :, h * HALF : (h + 1) * HALF])
+        for h in range(2):
+            nc.sync.dma_start(q_raw[h][:], query_v[:, :, h * HALF : (h + 1) * HALF])
+        nc.sync.dma_start(m_raw[0][:], msgs_v[:, :, 0:HALF])
+        nc.sync.dma_start(qs4[:], qs.rearrange("(p r) o -> p (r o)", r=PACK))
+        nc.sync.dma_start(fade_cols[:], fade.rearrange("o (h p j) -> p (o h) j", h=2, j=PACK))
+        nc.sync.dma_start(list3[:], offs3)
+        nc.sync.dma_start(m_raw[1][:], msgs_v[:, :, HALF : 2 * HALF])
+        for t in range(E // P):
+            nc.sync.dma_start(rows[t][:], old[t * P : (t + 1) * P, :])
+
+        k_codes = tile([P, I], U16, "k_codes")
+        k_scales = tile([P, I], U8, "k_scales")
+        nc.vector.tensor_copy(k_codes[:], key_words[:].indirect(list1[:]))
+
+        n_planes = tile([P, PACK, I], BF16, "n_planes")
+        for j in range(PACK):
+            if j % 2 == 0:
+                nc.scalar.activation(n_planes[:, j, :], note_planes[j][:].indirect(list2[:]), COPY)
+            else:
+                nc.vector.tensor_copy(n_planes[:, j, :], note_planes[j][:].indirect(list2[:]))
+            if j == 1:
+                nc.vector.tensor_copy(k_scales[:], key_scales[:].indirect(list1[:]))
+        n_words = tile([P, I, PACK], BF16, "n_words")
+        nc.vector.tensor_copy(
+            n_words[:].rearrange("p (c x) j -> p c j x", x=8), n_planes[:].rearrange("p j (c x) -> p c j x", x=8)
+        )
+        n_codes = tile([P, I], U32, "n_codes")
+        n_scales = tile([P, I], U8, "n_scales")
+        nc.vector.quantize_mx(n_codes[:].bitcast(FP8X4), n_scales[:], n_words[:].rearrange("p c j -> p (c j)"))
+
+        q2_words = tile([P, PACK, P, PACK], BF16, "q2_words")
+        for h in range(2):
+            nc.scalar.copy(
+                q2_words[:, :, 64 * h : 64 * (h + 1), :].rearrange("p r s j -> p s j r"),
+                q2_raw[h][:].rearrange("p j (s r) -> p s j r", r=PACK),
+            )
+        q2_codes = tile([P, Q], U32, "q2_codes")
+        q2_scales = tile([P, Q], U8, "q2_scales")
+        nc.vector.quantize_mx(q2_codes[:].bitcast(FP8X4), q2_scales[:], q2_words[:].rearrange("p r s j -> p (r s j)"))
+
+        scores = [ps.tile([P, PACK, CHUNK], F32, name=f"scores{c}") for c in range(CHUNKS)]
+        for c in range(CHUNKS):
+            slots = slice(c * CHUNK, (c + 1) * CHUNK)
+            for r in range(PACK):
+                cols = slice(r * P, (r + 1) * P)
+                nc.tensor.matmul_mx(
+                    scores[c][:, r, :],
+                    lhsT=q2_codes[:, cols].bitcast(FP8X4),
+                    lhsT_scale=q2_scales[:, cols],
+                    rhs=n_codes[:, slots].bitcast(FP8X4),
+                    rhs_scale=n_scales[:, slots],
+                    start=(r == 0),
+                    stop=False,
+                )
+
+        q_codes = tile([P, Q], U32, "q_codes")
+        q_scales = tile([P, Q], U8, "q_scales")
+        for h in range(2):
+            q_words = tile([P, PACK, 64, PACK], BF16, f"q_words{h}")
+            nc.vector.tensor_copy(
+                q_words[:].rearrange("p r s j -> p s j r"), q_raw[h][:].rearrange("p j (s r) -> p s j r", r=PACK)
+            )
+            for r in range(PACK):
+                cols = slice(r * P + 64 * h, r * P + 64 * (h + 1))
+                nc.vector.quantize_mx(
+                    q_codes[:, cols].bitcast(FP8X4), q_scales[:, cols], q_words[:, r, :, :].rearrange("p s j -> p (s j)")
+                )
+
+        for c in range(CHUNKS):
+            slots = slice(c * CHUNK, (c + 1) * CHUNK)
+            for r in range(PACK):
+                cols = slice(r * P, (r + 1) * P)
+                nc.tensor.matmul_mx(
+                    scores[c][:, r, :],
+                    lhsT=q_codes[:, cols].bitcast(FP8X4),
+                    lhsT_scale=q_scales[:, cols],
+                    rhs=k_codes[:, slots].bitcast(FP4X4),
+                    rhs_scale=k_scales[:, slots],
+                    start=False,
+                    stop=(r == PACK - 1),
+                )
+
+        fade_banks = [ps.tile([P, PACK, P], F32, name=f"fade_bank{h}") for h in range(2)]
+        for h in range(2):
+            for j in range(PACK):
+                nc.tensor.transpose(fade_banks[h][:, j, :], fade_cols[:, h, j : j + 1].to_broadcast([P, P]), ident[:])
+
+        m_codes = []
+        m_scales = []
+        for h in range(2):
+            m_words = tile([P, HALF, PACK], BF16, f"m_words{h}")
+            (nc.scalar.copy if h == 0 else nc.vector.tensor_copy)(
+                m_words[:].rearrange("p (c x) j -> p c j x", x=4), m_raw[h][:].rearrange("p j (c x) -> p c j x", x=4)
+            )
+            m_codes.append(tile([P, HALF], U32, f"m_codes{h}"))
+            m_scales.append(tile([P, HALF], U8, f"m_scales{h}"))
+            nc.vector.quantize_mx(
+                m_codes[h][:].bitcast(FP8X4), m_scales[h][:], m_words[:].rearrange("p c j -> p (c j)")
+            )
+
+        sums = tile([P, E // P, I], F32, "sums")
+
+        def scatter(engine, t, first, count):
+            target = windows[t][:].indirect(list3[:, first // 16 : (first + count) // 16])
+            source = sums[:, t, first : first + count]
+            if engine == "scalar":
+                nc.scalar.activation(target, source, COPY)
+            else:
+                nc.vector.tensor_copy(target, source)
+
+        weights = []
+        for c in range(CHUNKS):
+            w = tile([P, CHUNK, PACK], F32, f"w{c}")
+            nc.scalar.activation(w[:], scores[c][:].rearrange("p r i -> p i r"), SIGMOID)
+            weights.append(w)
+        for c in range(CHUNKS):
+            wq = tile([P, CHUNK, PACK], BF16, f"wq{c}")
+            nc.vector.tensor_tensor(wq[:], weights[c][:], qs4[:].unsqueeze(1).to_broadcast([P, CHUNK, PACK]), MULT)
+            w_codes = tile([P, CHUNK], U32, f"w_codes{c}")
+            w_scales = tile([P, CHUNK], U8, f"w_scales{c}")
+            nc.vector.quantize_mx(w_codes[:].bitcast(FP8X4), w_scales[:], wq[:].rearrange("p i r -> p (i r)"))
+            bank = ps2.tile([P, E // P, CHUNK], F32, name="sums_bank")
+            for t in range(E // P):
+                cols = slice((t % 2) * P, (t % 2 + 1) * P)
+                nc.tensor.matmul_mx(
+                    bank[:, t, :],
+                    lhsT=m_codes[t // 2][:, cols].bitcast(FP8X4),
+                    lhsT_scale=m_scales[t // 2][:, cols],
+                    rhs=w_codes[:].bitcast(FP8X4),
+                    rhs_scale=w_scales[:],
+                    start=True,
+                    stop=True,
+                )
+            nc.scalar.copy(sums[:, :, c * CHUNK : (c + 1) * CHUNK], bank[:])
+        for c in range(CHUNKS):
+            scatter("scalar", 0, c * CHUNK, CHUNK)
+        scatter("vector", 3, 2 * CHUNK, CHUNK)
+        scatter("vector", 3, 0, 2 * CHUNK)
+        scatter("vector", 3, 3 * CHUNK, CHUNK)
+        for t in (1, 2):
+            scatter("scalar", t, HALF, HALF)
+            scatter("scalar", t, 0, HALF)
+
+        for t in (0, 3, 1, 2):
+            for h in range(2):
+                cols = slice(h * BANK, (h + 1) * BANK)
+                half_row = rows[t][:, cols].rearrange("p (s j) -> p s j", j=PACK)
+                nc.vector.tensor_tensor(half_row, half_row, fade_banks[h][:].rearrange("p j s -> p s j"), MULT)
+        for t in (0, 3, 1, 2):
+            pieces = 2 if t == 2 else 1
+            for h in range(pieces):
+                cols = slice(h * M // pieces, (h + 1) * M // pieces)
+                nc.vector.tensor_tensor(rows[t][:, cols], rows[t][:, cols], windows[t][:, cols], ADD)
+                nc.sync.dma_start(out[t * P : (t + 1) * P, cols], rows[t][:, cols])

@@ -47,24 +47,29 @@ def tile_attend_twosources_delivered_lean_kernel(
         note_planes = [tile([P, U], F32, f"note_plane{j}") for j in range(PACK)]
         q2_raw = [tile([P, PACK, HALF], F32, f"q2_raw{h}") for h in range(2)]
         q_raw = [tile([P, PACK, HALF], F32, f"q_raw{h}") for h in range(2)]
-        m_raw = [tile([P, PACK, HALF], F32, f"m_raw{h}") for h in range(2)]
+        m_raw = tile([P, PACK, E], F32, "m_raw")
         rows = [tile([P, M], F32, f"rows{t}") for t in range(E // P)]
         windows = [tile([P, M], F32, f"window{t}") for t in range(E // P)]
-        qs4 = tile([P, PACK], F32, "qs4")
-        fade_cols = tile([P, 2, PACK], F32, "fade_cols")
+        vec_rows = tile([P, P], F32, "vec_rows")
+        vec_cols = tile([P, 8], F32, "vec_cols")
         ident = tile([P, P], F32, "ident")
 
         nc.vector.memset(key_scales[:].bitcast(I32), 0)
         for t in (0, 3):
             nc.vector.memset(windows[t][:], 0.0)
+        nc.gpsimd.memset(vec_rows[:], 0.0)
         make_identity(nc, ident[:])
+        nc.gpsimd.dma_start(vec_rows[0:8, :], fade.rearrange("o (j p) -> (o j) p", p=P))
+        nc.gpsimd.dma_start(
+            vec_rows[8:12, :].rearrange("r (g a) -> r g a", a=8), qs.rearrange("(g r a) o -> r g (a o)", r=PACK, a=8)
+        )
         for t in (1, 2):
             nc.gpsimd.memset(windows[t][:], 0.0)
 
         notes_v = notes.rearrange("(p j) u -> p j u", j=PACK)
         query_v = query.rearrange("(p j) q -> p j q", j=PACK)
         query2_v = query2.rearrange("(p j) q -> p j q", j=PACK)
-        msgs_v = msgs.rearrange("(p j) e -> p j e", j=PACK)
+        msgs_v = msgs.rearrange("(g r a) e -> r g a e", r=PACK, a=8)
         nc.sync.dma_start(list1[:], offs)
         nc.sync.dma_start(key_words[:].bitcast(I32), keys_words[0].bitcast(I32))
         nc.sync.dma_start(list2[:], offs2)
@@ -78,11 +83,9 @@ def tile_attend_twosources_delivered_lean_kernel(
             nc.sync.dma_start(q2_raw[h][:], query2_v[:, :, h * HALF : (h + 1) * HALF])
         for h in range(2):
             nc.sync.dma_start(q_raw[h][:], query_v[:, :, h * HALF : (h + 1) * HALF])
-        nc.sync.dma_start(m_raw[0][:], msgs_v[:, :, 0:HALF])
-        nc.sync.dma_start(qs4[:], qs.rearrange("(p r) o -> p (r o)", r=PACK))
-        nc.sync.dma_start(fade_cols[:], fade.rearrange("o (h p j) -> p (o h) j", h=2, j=PACK))
+        for r in range(PACK):
+            nc.sync.dma_start(m_raw[:, r, :], msgs_v[r])
         nc.sync.dma_start(list3[:], offs3)
-        nc.sync.dma_start(m_raw[1][:], msgs_v[:, :, HALF : 2 * HALF])
         for t in range(E // P):
             nc.sync.dma_start(rows[t][:], old[t * P : (t + 1) * P, :])
 
@@ -94,49 +97,49 @@ def tile_attend_twosources_delivered_lean_kernel(
         for j in range(PACK):
             if j % 2 == 0:
                 nc.scalar.activation(n_planes[:, j, :], note_planes[j][:].indirect(list2[:]), COPY)
-            else:
+            elif j == 1:
                 nc.vector.tensor_copy(n_planes[:, j, :], note_planes[j][:].indirect(list2[:]))
+            else:
+                nc.vector.tensor_copy(n_planes[:, j, 0:HALF], note_planes[j][:].indirect(list2[:, 0:16]))
+                nc.scalar.activation(n_planes[:, j, HALF:I], note_planes[j][:].indirect(list2[:, 16:32]), COPY)
             if j == 1:
                 nc.vector.tensor_copy(k_scales[:], key_scales[:].indirect(list1[:]))
         n_words = tile([P, I, PACK], BF16, "n_words")
         nc.vector.tensor_copy(
-            n_words[:].rearrange("p (c x) j -> p c j x", x=8), n_planes[:].rearrange("p j (c x) -> p c j x", x=8)
+            n_words[:], n_planes[:].rearrange("p j c -> p c j")
         )
         n_codes = tile([P, I], U32, "n_codes")
         n_scales = tile([P, I], U8, "n_scales")
         nc.vector.quantize_mx(n_codes[:].bitcast(FP8X4), n_scales[:], n_words[:].rearrange("p c j -> p (c j)"))
 
+        vec_bank = ps.tile([P, P], F32, name="vec_bank")
+        nc.tensor.transpose(vec_bank[:], vec_rows[:], ident[:])
+        nc.scalar.copy(vec_cols[:], vec_bank[:, 0:8])
+        fade_banks = []
+        for h in range(2):
+            bank = ps.tile([P, PACK, P], F32, name=f"fade_bank{h}")
+            for j in range(PACK):
+                column = PACK * h + j
+                nc.tensor.transpose(bank[:, j, :], vec_cols[:, column : column + 1].to_broadcast([P, P]), ident[:])
+            fade_banks.append(bank)
+
         q2_words = tile([P, PACK, P, PACK], BF16, "q2_words")
         for h in range(2):
             nc.scalar.copy(
-                q2_words[:, :, 64 * h : 64 * (h + 1), :].rearrange("p r s j -> p s j r"),
-                q2_raw[h][:].rearrange("p j (s r) -> p s j r", r=PACK),
+                q2_words[:, :, 64 * h : 64 * (h + 1), :].rearrange("p r (g a) j -> p g r a j", a=8),
+                q2_raw[h][:].rearrange("p j (g r a) -> p g r a j", r=PACK, a=8),
             )
         q2_codes = tile([P, Q], U32, "q2_codes")
         q2_scales = tile([P, Q], U8, "q2_scales")
         nc.vector.quantize_mx(q2_codes[:].bitcast(FP8X4), q2_scales[:], q2_words[:].rearrange("p r s j -> p (r s j)"))
 
-        scores = [ps.tile([P, PACK, CHUNK], F32, name=f"scores{c}") for c in range(CHUNKS)]
-        for c in range(CHUNKS):
-            slots = slice(c * CHUNK, (c + 1) * CHUNK)
-            for r in range(PACK):
-                cols = slice(r * P, (r + 1) * P)
-                nc.tensor.matmul_mx(
-                    scores[c][:, r, :],
-                    lhsT=q2_codes[:, cols].bitcast(FP8X4),
-                    lhsT_scale=q2_scales[:, cols],
-                    rhs=n_codes[:, slots].bitcast(FP8X4),
-                    rhs_scale=n_scales[:, slots],
-                    start=(r == 0),
-                    stop=False,
-                )
-
         q_codes = tile([P, Q], U32, "q_codes")
         q_scales = tile([P, Q], U8, "q_scales")
         for h in range(2):
             q_words = tile([P, PACK, 64, PACK], BF16, f"q_words{h}")
-            nc.vector.tensor_copy(
-                q_words[:].rearrange("p r s j -> p s j r"), q_raw[h][:].rearrange("p j (s r) -> p s j r", r=PACK)
+            (nc.scalar.copy if h == 0 else nc.vector.tensor_copy)(
+                q_words[:].rearrange("p r (g a) j -> p g r a j", a=8),
+                q_raw[h][:].rearrange("p j (g r a) -> p g r a j", r=PACK, a=8),
             )
             for r in range(PACK):
                 cols = slice(r * P + 64 * h, r * P + 64 * (h + 1))
@@ -144,37 +147,17 @@ def tile_attend_twosources_delivered_lean_kernel(
                     q_codes[:, cols].bitcast(FP8X4), q_scales[:, cols], q_words[:, r, :, :].rearrange("p s j -> p (s j)")
                 )
 
-        for c in range(CHUNKS):
-            slots = slice(c * CHUNK, (c + 1) * CHUNK)
-            for r in range(PACK):
-                cols = slice(r * P, (r + 1) * P)
-                nc.tensor.matmul_mx(
-                    scores[c][:, r, :],
-                    lhsT=q_codes[:, cols].bitcast(FP8X4),
-                    lhsT_scale=q_scales[:, cols],
-                    rhs=k_codes[:, slots].bitcast(FP4X4),
-                    rhs_scale=k_scales[:, slots],
-                    start=False,
-                    stop=(r == PACK - 1),
-                )
+        m_words = [tile([P, HALF, PACK], BF16, f"m_words{h}") for h in range(2)]
+        m_codes = [tile([P, HALF], U32, f"m_codes{h}") for h in range(2)]
+        m_scales = [tile([P, HALF], U8, f"m_scales{h}") for h in range(2)]
 
-        fade_banks = [ps.tile([P, PACK, P], F32, name=f"fade_bank{h}") for h in range(2)]
-        for h in range(2):
-            for j in range(PACK):
-                nc.tensor.transpose(fade_banks[h][:, j, :], fade_cols[:, h, j : j + 1].to_broadcast([P, P]), ident[:])
-
-        m_codes = []
-        m_scales = []
-        for h in range(2):
-            m_words = tile([P, HALF, PACK], BF16, f"m_words{h}")
-            (nc.scalar.copy if h == 0 else nc.vector.tensor_copy)(
-                m_words[:].rearrange("p (c x) j -> p c j x", x=4), m_raw[h][:].rearrange("p j (c x) -> p c j x", x=4)
-            )
-            m_codes.append(tile([P, HALF], U32, f"m_codes{h}"))
-            m_scales.append(tile([P, HALF], U8, f"m_scales{h}"))
+        def msgs_half(h, copy):
+            copy(m_words[h][:], m_raw[:, :, h * HALF : (h + 1) * HALF].rearrange("p r e -> p e r"))
             nc.vector.quantize_mx(
-                m_codes[h][:].bitcast(FP8X4), m_scales[h][:], m_words[:].rearrange("p c j -> p (c j)")
+                m_codes[h][:].bitcast(FP8X4), m_scales[h][:], m_words[h][:].rearrange("p c j -> p (c j)")
             )
+
+        msgs_half(0, nc.vector.tensor_copy)
 
         sums = tile([P, E // P, I], F32, "sums")
 
@@ -188,16 +171,42 @@ def tile_attend_twosources_delivered_lean_kernel(
 
         weights = []
         for c in range(CHUNKS):
+            slots = slice(c * CHUNK, (c + 1) * CHUNK)
+            scores = ps2.tile([P, PACK, CHUNK], F32, name="scores")
+            for r in range(PACK):
+                cols = slice(r * P, (r + 1) * P)
+                nc.tensor.matmul_mx(
+                    scores[:, r, :],
+                    lhsT=q2_codes[:, cols].bitcast(FP8X4),
+                    lhsT_scale=q2_scales[:, cols],
+                    rhs=n_codes[:, slots].bitcast(FP8X4),
+                    rhs_scale=n_scales[:, slots],
+                    start=(r == 0),
+                    stop=False,
+                )
+            for r in range(PACK):
+                cols = slice(r * P, (r + 1) * P)
+                nc.tensor.matmul_mx(
+                    scores[:, r, :],
+                    lhsT=q_codes[:, cols].bitcast(FP8X4),
+                    lhsT_scale=q_scales[:, cols],
+                    rhs=k_codes[:, slots].bitcast(FP4X4),
+                    rhs_scale=k_scales[:, slots],
+                    start=False,
+                    stop=(r == PACK - 1),
+                )
             w = tile([P, CHUNK, PACK], F32, f"w{c}")
-            nc.scalar.activation(w[:], scores[c][:].rearrange("p r i -> p i r"), SIGMOID)
+            nc.scalar.activation(w[:], scores[:].rearrange("p r i -> p i r"), SIGMOID)
             weights.append(w)
+            if c == 1:
+                msgs_half(1, nc.scalar.copy)
         for c in range(CHUNKS):
             wq = tile([P, CHUNK, PACK], BF16, f"wq{c}")
-            nc.vector.tensor_tensor(wq[:], weights[c][:], qs4[:].unsqueeze(1).to_broadcast([P, CHUNK, PACK]), MULT)
+            nc.vector.tensor_tensor(wq[:], weights[c][:], vec_bank[:, 8:12].unsqueeze(1).to_broadcast([P, CHUNK, PACK]), MULT)
             w_codes = tile([P, CHUNK], U32, f"w_codes{c}")
             w_scales = tile([P, CHUNK], U8, f"w_scales{c}")
             nc.vector.quantize_mx(w_codes[:].bitcast(FP8X4), w_scales[:], wq[:].rearrange("p i r -> p (i r)"))
-            bank = ps2.tile([P, E // P, CHUNK], F32, name="sums_bank")
+            bank = ps.tile([P, E // P, CHUNK], F32, name=f"sums_bank{c % 3}")
             for t in range(E // P):
                 cols = slice((t % 2) * P, (t % 2 + 1) * P)
                 nc.tensor.matmul_mx(
@@ -214,7 +223,7 @@ def tile_attend_twosources_delivered_lean_kernel(
             scatter("scalar", 0, c * CHUNK, CHUNK)
         scatter("vector", 3, 2 * CHUNK, CHUNK)
         scatter("vector", 3, 0, 2 * CHUNK)
-        scatter("vector", 3, 3 * CHUNK, CHUNK)
+        scatter("scalar", 3, 3 * CHUNK, CHUNK)
         for t in (1, 2):
             scatter("scalar", t, HALF, HALF)
             scatter("scalar", t, 0, HALF)
@@ -222,8 +231,7 @@ def tile_attend_twosources_delivered_lean_kernel(
         for t in (0, 3, 1, 2):
             for h in range(2):
                 cols = slice(h * BANK, (h + 1) * BANK)
-                half_row = rows[t][:, cols].rearrange("p (s j) -> p s j", j=PACK)
-                nc.vector.tensor_tensor(half_row, half_row, fade_banks[h][:].rearrange("p j s -> p s j"), MULT)
+                nc.vector.tensor_tensor(rows[t][:, cols], rows[t][:, cols], fade_banks[h][:].rearrange("p j s -> p (j s)"), MULT)
         for t in (0, 3, 1, 2):
             pieces = 2 if t == 2 else 1
             for h in range(pieces):

from contextlib import ExitStack

import concourse.mybir as mybir
from concourse.masks import make_identity

D, T, I, Q, E, U, M = 512, 2048, 512, 512, 512, 1024, 1024
FLOPS = 2 * (2 * D * Q * I + Q * E * I)

F32 = mybir.dt.float32
BF16 = mybir.dt.bfloat16
I32 = mybir.dt.int32
U32 = mybir.dt.uint32
U16 = mybir.dt.uint16
U8 = mybir.dt.uint8
FP8X4 = mybir.dt.float8_e4m3fn_x4
FP4X4 = mybir.dt.float4_e2m1fn_x4
MULT = mybir.AluOpType.mult
ADD = mybir.AluOpType.add
COPY = mybir.ActivationFunctionType.Copy
SIGMOID = mybir.ActivationFunctionType.Sigmoid

P = 128
PACK = 4
CHUNK = 128
CHUNKS = I // CHUNK
HALF = 256
BANK = 512


def tile_attend_twosources_delivered_lean_kernel(
    tc, query, query2, keys_words, keys_scales, notes, qs, msgs, old, fade, offs, offs2, offs3, out
):
    nc = tc.nc
    with ExitStack() as ctx:
        sb = ctx.enter_context(tc.tile_pool(name="sb", bufs=1))
        ps = ctx.enter_context(tc.psum_pool(name="ps", bufs=1))
        ps2 = ctx.enter_context(tc.psum_pool(name="ps2", bufs=2))

        def tile(shape, dtype, name):
            return sb.tile(shape, dtype, name=name, align_bytes=64)

        list1 = tile([P, I // 16], U16, "list1")
        list2 = tile([P, I // 16], U16, "list2")
        list3 = tile([P, I // 16], U16, "list3")
        key_words = tile([P, T], U16, "key_words")
        key_scales = tile([P, T], U8, "key_scales")
        note_planes = [tile([P, U], F32, f"note_plane{j}") for j in range(PACK)]
        q2_raw = [tile([P, PACK, HALF], F32, f"q2_raw{h}") for h in range(2)]
        q_raw = [tile([P, PACK, HALF], F32, f"q_raw{h}") for h in range(2)]
        m_raw = tile([P, PACK, E], F32, "m_raw")
        rows = [tile([P, M], F32, f"rows{t}") for t in range(E // P)]
        windows = [tile([P, M], F32, f"window{t}") for t in range(E // P)]
        vec_rows = tile([P, P], F32, "vec_rows")
        vec_cols = tile([P, 8], F32, "vec_cols")
        ident = tile([P, P], F32, "ident")

        nc.vector.memset(key_scales[:].bitcast(I32), 0)
        for t in (0, 3):
            nc.vector.memset(windows[t][:], 0.0)
        nc.gpsimd.memset(vec_rows[:], 0.0)
        make_identity(nc, ident[:])
        nc.gpsimd.dma_start(vec_rows[0:8, :], fade.rearrange("o (j p) -> (o j) p", p=P))
        nc.gpsimd.dma_start(
            vec_rows[8:12, :].rearrange("r (g a) -> r g a", a=8), qs.rearrange("(g r a) o -> r g (a o)", r=PACK, a=8)
        )
        for t in (1, 2):
            nc.gpsimd.memset(windows[t][:], 0.0)

        notes_v = notes.rearrange("(p j) u -> p j u", j=PACK)
        query_v = query.rearrange("(p j) q -> p j q", j=PACK)
        query2_v = query2.rearrange("(p j) q -> p j q", j=PACK)
        msgs_v = msgs.rearrange("(g r a) e -> r g a e", r=PACK, a=8)
        nc.sync.dma_start(list1[:], offs)
        nc.sync.dma_start(key_words[:].bitcast(I32), keys_words[0].bitcast(I32))
        nc.sync.dma_start(list2[:], offs2)
        for j in range(PACK):
            nc.sync.dma_start(note_planes[j][:], notes_v[:, j, :])
        for g in range(4):
            nc.scalar.dma_start(
                key_scales[32 * g : 32 * g + 4, :].bitcast(I32), keys_scales[0, 4 * g : 4 * g + 4, :].bitcast(I32)
            )
        for h in range(2):
            nc.sync.dma_start(q2_raw[h][:], query2_v[:, :, h * HALF : (h + 1) * HALF])
        for h in range(2):
            nc.sync.dma_start(q_raw[h][:], query_v[:, :, h * HALF : (h + 1) * HALF])
        for r in range(PACK):
            nc.sync.dma_start(m_raw[:, r, :], msgs_v[r])
        nc.sync.dma_start(list3[:], offs3)
        for t in range(E // P):
            nc.sync.dma_start(rows[t][:], old[t * P : (t + 1) * P, :])

        k_codes = tile([P, I], U16, "k_codes")
        k_scales = tile([P, I], U8, "k_scales")
        nc.vector.tensor_copy(k_codes[:], key_words[:].indirect(list1[:]))

        n_planes = tile([P, PACK, I], BF16, "n_planes")
        for j in range(PACK):
            if j % 2 == 0:
                nc.scalar.activation(n_planes[:, j, :], note_planes[j][:].indirect(list2[:]), COPY)
            elif j == 1:
                nc.vector.tensor_copy(n_planes[:, j, :], note_planes[j][:].indirect(list2[:]))
            else:
                nc.vector.tensor_copy(n_planes[:, j, 0:HALF], note_planes[j][:].indirect(list2[:, 0:16]))
                nc.scalar.activation(n_planes[:, j, HALF:I], note_planes[j][:].indirect(list2[:, 16:32]), COPY)
            if j == 1:
                nc.vector.tensor_copy(k_scales[:], key_scales[:].indirect(list1[:]))
        n_words = tile([P, I, PACK], BF16, "n_words")
        nc.vector.tensor_copy(
            n_words[:], n_planes[:].rearrange("p j c -> p c j")
        )
        n_codes = tile([P, I], U32, "n_codes")
        n_scales = tile([P, I], U8, "n_scales")
        nc.vector.quantize_mx(n_codes[:].bitcast(FP8X4), n_scales[:], n_words[:].rearrange("p c j -> p (c j)"))

        vec_bank = ps.tile([P, P], F32, name="vec_bank")
        nc.tensor.transpose(vec_bank[:], vec_rows[:], ident[:])
        nc.scalar.copy(vec_cols[:], vec_bank[:, 0:8])
        fade_banks = []
        for h in range(2):
            bank = ps.tile([P, PACK, P], F32, name=f"fade_bank{h}")
            for j in range(PACK):
                column = PACK * h + j
                nc.tensor.transpose(bank[:, j, :], vec_cols[:, column : column + 1].to_broadcast([P, P]), ident[:])
            fade_banks.append(bank)

        q2_words = tile([P, PACK, P, PACK], BF16, "q2_words")
        for h in range(2):
            nc.scalar.copy(
                q2_words[:, :, 64 * h : 64 * (h + 1), :].rearrange("p r (g a) j -> p g r a j", a=8),
                q2_raw[h][:].rearrange("p j (g r a) -> p g r a j", r=PACK, a=8),
            )
        q2_codes = tile([P, Q], U32, "q2_codes")
        q2_scales = tile([P, Q], U8, "q2_scales")
        nc.vector.quantize_mx(q2_codes[:].bitcast(FP8X4), q2_scales[:], q2_words[:].rearrange("p r s j -> p (r s j)"))

        q_codes = tile([P, Q], U32, "q_codes")
        q_scales = tile([P, Q], U8, "q_scales")
        for h in range(2):
            q_words = tile([P, PACK, 64, PACK], BF16, f"q_words{h}")
            (nc.scalar.copy if h == 0 else nc.vector.tensor_copy)(
                q_words[:].rearrange("p r (g a) j -> p g r a j", a=8),
                q_raw[h][:].rearrange("p j (g r a) -> p g r a j", r=PACK, a=8),
            )
            for r in range(PACK):
                cols = slice(r * P + 64 * h, r * P + 64 * (h + 1))
                nc.vector.quantize_mx(
                    q_codes[:, cols].bitcast(FP8X4), q_scales[:, cols], q_words[:, r, :, :].rearrange("p s j -> p (s j)")
                )

        m_words = [tile([P, HALF, PACK], BF16, f"m_words{h}") for h in range(2)]
        m_codes = [tile([P, HALF], U32, f"m_codes{h}") for h in range(2)]
        m_scales = [tile([P, HALF], U8, f"m_scales{h}") for h in range(2)]

        def msgs_half(h, copy):
            copy(m_words[h][:], m_raw[:, :, h * HALF : (h + 1) * HALF].rearrange("p r e -> p e r"))
            nc.vector.quantize_mx(
                m_codes[h][:].bitcast(FP8X4), m_scales[h][:], m_words[h][:].rearrange("p c j -> p (c j)")
            )

        msgs_half(0, nc.vector.tensor_copy)

        sums = tile([P, E // P, I], F32, "sums")

        def scatter(engine, t, first, count):
            target = windows[t][:].indirect(list3[:, first // 16 : (first + count) // 16])
            source = sums[:, t, first : first + count]
            if engine == "scalar":
                nc.scalar.activation(target, source, COPY)
            else:
                nc.vector.tensor_copy(target, source)

        weights = []
        for c in range(CHUNKS):
            slots = slice(c * CHUNK, (c + 1) * CHUNK)
            scores = ps2.tile([P, PACK, CHUNK], F32, name="scores")
            for r in range(PACK):
                cols = slice(r * P, (r + 1) * P)
                nc.tensor.matmul_mx(
                    scores[:, r, :],
                    lhsT=q2_codes[:, cols].bitcast(FP8X4),
                    lhsT_scale=q2_scales[:, cols],
                    rhs=n_codes[:, slots].bitcast(FP8X4),
                    rhs_scale=n_scales[:, slots],
                    start=(r == 0),
                    stop=False,
                )
            for r in range(PACK):
                cols = slice(r * P, (r + 1) * P)
                nc.tensor.matmul_mx(
                    scores[:, r, :],
                    lhsT=q_codes[:, cols].bitcast(FP8X4),
                    lhsT_scale=q_scales[:, cols],
                    rhs=k_codes[:, slots].bitcast(FP4X4),
                    rhs_scale=k_scales[:, slots],
                    start=False,
                    stop=(r == PACK - 1),
                )
            w = tile([P, CHUNK, PACK], F32, f"w{c}")
            nc.scalar.activation(w[:], scores[:].rearrange("p r i -> p i r"), SIGMOID)
            weights.append(w)
            if c == 1:
                msgs_half(1, nc.scalar.copy)
        for c in range(CHUNKS):
            wq = tile([P, CHUNK, PACK], BF16, f"wq{c}")
            nc.vector.tensor_tensor(wq[:], weights[c][:], vec_bank[:, 8:12].unsqueeze(1).to_broadcast([P, CHUNK, PACK]), MULT)
            w_codes = tile([P, CHUNK], U32, f"w_codes{c}")
            w_scales = tile([P, CHUNK], U8, f"w_scales{c}")
            nc.vector.quantize_mx(w_codes[:].bitcast(FP8X4), w_scales[:], wq[:].rearrange("p i r -> p (i r)"))
            bank = ps.tile([P, E // P, CHUNK], F32, name=f"sums_bank{c % 3}")
            for t in range(E // P):
                cols = slice((t % 2) * P, (t % 2 + 1) * P)
                nc.tensor.matmul_mx(
                    bank[:, t, :],
                    lhsT=m_codes[t // 2][:, cols].bitcast(FP8X4),
                    lhsT_scale=m_scales[t // 2][:, cols],
                    rhs=w_codes[:].bitcast(FP8X4),
                    rhs_scale=w_scales[:],
                    start=True,
                    stop=True,
                )
            nc.scalar.copy(sums[:, :, c * CHUNK : (c + 1) * CHUNK], bank[:])
        for c in range(CHUNKS):
            scatter("scalar", 0, c * CHUNK, CHUNK)
        scatter("vector", 3, 2 * CHUNK, CHUNK)
        scatter("vector", 3, 0, 2 * CHUNK)
        scatter("scalar", 3, 3 * CHUNK, CHUNK)
        for t in (1, 2):
            scatter("scalar", t, HALF, HALF)
            scatter("scalar", t, 0, HALF)

        for t in (0, 3, 1, 2):
            for h in range(2):
                cols = slice(h * BANK, (h + 1) * BANK)
                nc.vector.tensor_tensor(rows[t][:, cols], rows[t][:, cols], fade_banks[h][:].rearrange("p j s -> p (j s)"), MULT)
        for t in (0, 3, 1, 2):
            pieces = 2 if t == 2 else 1
            for h in range(pieces):
                cols = slice(h * M // pieces, (h + 1) * M // pieces)
                nc.vector.tensor_tensor(rows[t][:, cols], rows[t][:, cols], windows[t][:, cols], ADD)
                nc.sync.dma_start(out[t * P : (t + 1) * P, cols], rows[t][:, cols])
